import numpy as np
import ml_dtypes


def mxq(x, axis, fmt="e4m3"):
    dtype, down = {"e4m3": (ml_dtypes.float8_e4m3fn, 7), "e5m2": (ml_dtypes.float8_e5m2, 14)}[fmt]
    v = np.moveaxis(np.asarray(x, np.float32).astype(ml_dtypes.bfloat16).astype(np.float64), axis, -1)
    blocks = v.reshape(v.shape[:-1] + (-1, 32))
    amax = np.abs(blocks).max(-1, keepdims=True)
    byte = np.maximum(np.where(amax > 0, np.frexp(amax)[1] - 1 + 127, 0) - down, 1)
    scale = np.exp2(byte - 127.0)
    codes = (blocks / scale).astype(np.float32).astype(dtype).astype(np.float64)
    return np.moveaxis((codes * scale).reshape(v.shape), -1, axis)


WIDE = False


def mx_kscale(k):
    if not WIDE:
        return np.ones(k)
    levels = np.array([10, -10, 5, -5, 0])
    if k % 512:
        return np.exp2(np.random.permutation(np.resize(levels, k // 32))).repeat(32)
    a = np.empty((k // 512, 16))
    for p in range(k // 512):
        a[p, :8] = np.random.permutation(np.resize(levels, 8))
        for g in range(8):
            far = levels[np.abs(levels - a[p, g]) >= 10]
            a[p, g + 8] = far[np.random.randint(len(far))]
    return np.exp2(a.ravel()).repeat(32)


def f64(x):
    return np.asarray(x).astype(np.float64)


def striped(idx):
    return np.tile(idx.reshape(-1, 16).T, (8, 1)).astype(np.uint16)


def unstriped(offs):
    return offs[:16].T.reshape(-1).astype(np.int64)


K, T, S, D, V, N = 512, 1024, 512, 4, 256, 128
P = 2 ** 7


def setup_inputs():
    n = np.random.standard_normal
    s = mx_kscale(K)[:, None]
    return {
        "xT": (n((K, T)) * s).astype(np.float32),
        "w1": (n((K, N)) / np.sqrt(K) / s).astype(np.float32),
        "score": np.tile(np.random.standard_normal((D, 1, V)), (1, P, 1)).astype(np.float32),
        "offs": striped(np.random.permutation(T)[:S]),
        "pos1": striped(np.random.permutation(S)[:V]),
        "pos2": striped(np.random.permutation(S)[:V]),
        "pos3": striped(np.random.permutation(S)[:V]),
        "pos4": striped(np.random.permutation(S)[:V]),
    }


def reference(xT, w1, score, offs, pos1, pos2, pos3, pos4):
    xq = mxq(f64(xT)[:, unstriped(offs)], 0, "e4m3")
    y = mxq(f64(w1), 0, "e4m3").T @ xq
    e0 = np.exp(f64(score)[0, :1])
    e1 = np.exp(f64(score)[1, :1])
    e2 = np.exp(f64(score)[2, :1])
    e3 = np.exp(f64(score)[3, :1])
    num = y[:, unstriped(pos1)] * e0 + y[:, unstriped(pos2)] * e1 + y[:, unstriped(pos3)] * e2 + y[:, unstriped(pos4)] * e3
    den = e0 + e1 + e2 + e3
    return num / den

@@ -1,0 +1,141 @@
+from contextlib import ExitStack
+
+import concourse.mybir as mybir
+from concourse.masks import make_identity
+
+K, T, S, D, V, N = 512, 1024, 512, 4, 256, 128
+FLOPS = 2 * K * S * N
+
+F32 = mybir.dt.float32
+BF16 = mybir.dt.bfloat16
+U32 = mybir.dt.uint32
+U16 = mybir.dt.uint16
+U8 = mybir.dt.uint8
+I32 = mybir.dt.int32
+FP8X4 = mybir.dt.float8_e4m3fn_x4
+ACT = mybir.ActivationFunctionType
+ALU = mybir.AluOpType
+AX = mybir.AxisListType
+
+P = 128
+PACK = 4
+PER_COL = 16
+
+PIECES = ((0, 256), (256, 128), (384, 128))
+CAST_SPLIT = 608
+
+
+def tile_picked_gatv_none_e_kernel(tc, xT, w1, score, offs, pos1, pos2, pos3, pos4, out):
+    nc = tc.nc
+    with ExitStack() as ctx:
+        keep = ctx.enter_context(tc.tile_pool(name="keep", bufs=1))
+        psum = ctx.enter_context(tc.psum_pool(name="psum", bufs=1))
+
+        x_rows = xT.rearrange("(p j) t -> p j t", j=PACK)
+        planes = [keep.tile([P, T], F32, name=f"plane{j}") for j in range(PACK)]
+        offs_sb = keep.tile([P, S // PER_COL], U16, name="offs_sb")
+        pos_sb = [keep.tile([P, V // PER_COL], U16, name=f"pos_sb{d}") for d in range(D)]
+        w_raw = keep.tile([P, PACK, N], F32, name="w_raw")
+        score_rows = keep.tile([P, P], F32, name="score_rows")
+        ident = keep.tile([P, P], F32, name="ident")
+
+        nc.sync.dma_start(planes[0][:], x_rows[:, 0, :])
+        nc.sync.dma_start(offs_sb[:], offs)
+        nc.sync.dma_start(w_raw[:], w1.rearrange("(p j) n -> p j n", j=PACK))
+        for j in (2, 1, 3):
+            nc.sync.dma_start(planes[j][:], x_rows[:, j, :])
+        for pos_tile, pos in zip(pos_sb, (pos1, pos2, pos3, pos4)):
+            nc.sync.dma_start(pos_tile[:], pos)
+
+        nc.gpsimd.memset(score_rows[:], 0.0)
+        nc.scalar.dma_start(score_rows[0:8, :], score[:, 0, :].rearrange("d (h c) -> d h c", h=2))
+        make_identity(nc, ident[:])
+
+        score_t = psum.tile([P, P], F32, name="score_t")
+        nc.tensor.transpose(score_t[:], score_rows[:], ident[:])
+        neg_max = keep.tile([P, 2], F32, name="neg_max")
+        nc.vector.tensor_reduce(neg_max[:], score_t[:, 0:8].rearrange("p (d h) -> p h d", h=2), AX.X, ALU.max, negate=True)
+        expd = keep.tile([P, 2, D], F32, name="expd", tag="half1")
+        den = keep.tile([P, 2], F32, name="den")
+        for h in range(2):
+            nc.scalar.activation(expd[:, h, :], score_t[:, h:8:2], ACT.Exp, bias=neg_max[:, h:h + 1], accum_out=den[:, h:h + 1])
+        inv_den = keep.tile([P, 2], F32, name="inv_den")
+        nc.vector.reciprocal(inv_den[:], den[:])
+        attn = keep.tile([P, 2, D], F32, name="attn")
+        nc.vector.tensor_tensor(attn[:], expd[:], inv_den[:].unsqueeze(2).to_broadcast([P, 2, D]), ALU.mult)
+        attn_banks = [psum.tile([P, 2 * V], F32, name=f"attn_bank{b}") for b in range(2)]
+        for d in range(D):
+            for h in range(2):
+                c0 = (d % 2) * V + h * P
+                nc.tensor.transpose(attn_banks[d // 2][:, c0:c0 + P], attn[:, h, d:d + 1].to_broadcast([P, P]), ident[:])
+
+        picked = [keep.tile([P, n, PACK], BF16, name=f"picked{i}", tag=f"picked{i}", align_bytes=64) for i, (s0, n) in enumerate(PIECES)]
+
+        def offsets(i):
+            s0, n = PIECES[i]
+            return offs_sb[:, s0 // PER_COL:(s0 + n) // PER_COL]
+
+        half = [keep.tile([P, T], BF16, name=f"half{j}", tag=f"half{j}") for j in range(2)]
+        nc.vector.tensor_copy(half[0][:], planes[0][:])
+        for i in range(len(PIECES)):
+            nc.scalar.activation(picked[i][:, :, 0], half[0][:].indirect(offsets(i)), ACT.Copy)
+        w_bf = keep.tile([P, N, PACK], BF16, name="w_bf", align_bytes=64)
+        nc.vector.tensor_copy(w_bf[:], w_raw[:].rearrange("p j n -> p n j"))
+        w_codes = keep.tile([P, N], U32, name="w_codes", align_bytes=64)
+        w_scales = keep.tile([P, N], U8, name="w_scales", align_bytes=64)
+        nc.vector.quantize_mx(out=w_codes[:].bitcast(FP8X4), scales=w_scales[:], in_=w_bf[:].rearrange("p n j -> p (n j)"))
+        for i in range(len(PIECES)):
+            nc.vector.tensor_copy(picked[i][:, :, 2], planes[2][:].indirect(offsets(i)))
+        nc.scalar.activation(half[1][:, :CAST_SPLIT], planes[1][:, :CAST_SPLIT], ACT.Copy)
+        nc.vector.tensor_copy(half[1][:, CAST_SPLIT:], planes[1][:, CAST_SPLIT:])
+        for i in range(len(PIECES)):
+            nc.scalar.activation(picked[i][:, :, 1], half[1][:].indirect(offsets(i)), ACT.Copy)
+
+        codes = [keep.tile([P, n], U32, name=f"codes{i}", align_bytes=64) for i, (s0, n) in enumerate(PIECES)]
+        scales = [keep.tile([P, n], U8, name=f"scales{i}", align_bytes=64) for i, (s0, n) in enumerate(PIECES)]
+
+        def gather_last(i):
+            nc.vector.tensor_copy(picked[i][:, :, 3], planes[3][:].indirect(offsets(i)))
+
+        def quantise(i):
+            nc.vector.quantize_mx(out=codes[i][:].bitcast(FP8X4), scales=scales[i][:], in_=picked[i][:].rearrange("p n j -> p (n j)"))
+
+        gather_last(0)
+        gather_last(1)
+        quantise(0)
+        gather_last(2)
+        quantise(1)
+        quantise(2)
+        attn_all = keep.tile([P, D * V], F32, name="attn_all", tag="picked2", align_bytes=64)
+        attn_sb = [attn_all[:, b * 2 * V:(b + 1) * 2 * V] for b in range(2)]
+        for b in range(2):
+            nc.vector.tensor_copy(attn_sb[b], attn_banks[b][:])
+
+        y = keep.tile([P, S], F32, name="y")
+        for i, (s0, n) in enumerate(PIECES):
+            acc = psum.tile([P, n], F32, name=f"acc{i}")
+            nc.tensor.matmul_mx(out=acc[:], lhsT=w_codes[:].bitcast(FP8X4), lhsT_scale=w_scales[:],
+                                rhs=codes[i][:].bitcast(FP8X4), rhs_scale=scales[i][:], start=True, stop=True)
+            nc.scalar.copy(y[:, s0:s0 + n], acc[:])
+
+        terms = [keep.tile([P, V], F32, name=f"term{d}") for d in range(D)]
+
+        def weighted(d, c0, n):
+            a0 = (d % 2) * V + c0
+            nc.vector.tensor_tensor(terms[d][:, c0:c0 + n], y[:].indirect(pos_sb[d][:, c0 // PER_COL:(c0 + n) // PER_COL]),
+                                    attn_sb[d // 2][:, a0:a0 + n], ALU.mult)
+
+        sum01 = keep.tile([P, V], F32, name="sum01")
+        sum012 = keep.tile([P, V], F32, name="sum012")
+        res = [keep.tile([P, P], F32, name=f"res{h}") for h in range(2)]
+        weighted(0, 0, V)
+        weighted(1, 0, V)
+        weighted(2, 0, V)
+        nc.vector.tensor_tensor(sum01[:], terms[0][:], terms[1][:], ALU.add)
+        weighted(3, 0, P)
+        nc.vector.tensor_tensor(sum012[:], sum01[:], terms[2][:], ALU.add)
+        weighted(3, P, P)
+        for h in range(2):
+            cols = slice(h * P, (h + 1) * P)
+            nc.vector.tensor_tensor(res[h][:], sum012[:, cols], terms[3][:, cols], ALU.add)
+            (nc.scalar if h == 0 else nc.sync).dma_start(out[:, cols], res[h][:])

@@ -22,7 +22,7 @@ PACK = 4
 PER_COL = 16
 
 PIECES = ((0, 256), (256, 128), (384, 128))
-CAST_SPLIT = 608
+SCORE_PAD = 8
 
 
 def tile_picked_gatv_none_e_kernel(tc, xT, w1, score, offs, pos1, pos2, pos3, pos4, out):
@@ -36,29 +36,31 @@ def tile_picked_gatv_none_e_kernel(tc, xT, w1, score, offs, pos1, pos2, pos3, po
         offs_sb = keep.tile([P, S // PER_COL], U16, name="offs_sb")
         pos_sb = [keep.tile([P, V // PER_COL], U16, name=f"pos_sb{d}") for d in range(D)]
         w_raw = keep.tile([P, PACK, N], F32, name="w_raw")
-        score_rows = keep.tile([P, P], F32, name="score_rows")
+        score_sb = keep.tile([P, D, SCORE_PAD], F32, name="score_sb")
         ident = keep.tile([P, P], F32, name="ident")
 
+        nc.scalar.dma_start(score_sb[:, :, 0:2], score[:, 0, :].rearrange("d (p h) -> p d h", h=2))
         nc.sync.dma_start(planes[0][:], x_rows[:, 0, :])
         nc.sync.dma_start(offs_sb[:], offs)
-        nc.sync.dma_start(w_raw[:], w1.rearrange("(p j) n -> p j n", j=PACK))
-        for j in (2, 1, 3):
+        for j in (1, 2):
             nc.sync.dma_start(planes[j][:], x_rows[:, j, :])
+        nc.sync.dma_start(w_raw[:], w1.rearrange("(p j) n -> p j n", j=PACK))
+        nc.sync.dma_start(planes[3][:], x_rows[:, 3, :])
         for pos_tile, pos in zip(pos_sb, (pos1, pos2, pos3, pos4)):
             nc.sync.dma_start(pos_tile[:], pos)
 
-        nc.gpsimd.memset(score_rows[:], 0.0)
-        nc.scalar.dma_start(score_rows[0:8, :], score[:, 0, :].rearrange("d (h c) -> d h c", h=2))
         make_identity(nc, ident[:])
+        warm_in = keep.tile([P, 1], F32, name="warm_in")
+        warm_out = keep.tile([P, 1], F32, name="warm_out")
+        nc.vector.memset(warm_in[:], 0.0)
+        nc.scalar.activation(warm_out[:], warm_in[:], ACT.Exp)
 
-        score_t = psum.tile([P, P], F32, name="score_t")
-        nc.tensor.transpose(score_t[:], score_rows[:], ident[:])
         neg_max = keep.tile([P, 2], F32, name="neg_max")
-        nc.vector.tensor_reduce(neg_max[:], score_t[:, 0:8].rearrange("p (d h) -> p h d", h=2), AX.X, ALU.max, negate=True)
-        expd = keep.tile([P, 2, D], F32, name="expd", tag="half1")
+        nc.vector.tensor_reduce(neg_max[:], score_sb[:, :, 0:2].rearrange("p d h -> p h d"), AX.X, ALU.max, negate=True)
+        expd = keep.tile([P, 2, D], F32, name="expd")
         den = keep.tile([P, 2], F32, name="den")
         for h in range(2):
-            nc.scalar.activation(expd[:, h, :], score_t[:, h:8:2], ACT.Exp, bias=neg_max[:, h:h + 1], accum_out=den[:, h:h + 1])
+            nc.scalar.activation(expd[:, h, :], score_sb[:, :, h], ACT.Exp, bias=neg_max[:, h:h + 1], accum_out=den[:, h:h + 1])
         inv_den = keep.tile([P, 2], F32, name="inv_den")
         nc.vector.reciprocal(inv_den[:], den[:])
         attn = keep.tile([P, 2, D], F32, name="attn")
@@ -75,41 +77,47 @@ def tile_picked_gatv_none_e_kernel(tc, xT, w1, score, offs, pos1, pos2, pos3, po
             s0, n = PIECES[i]
             return offs_sb[:, s0 // PER_COL:(s0 + n) // PER_COL]
 
-        half = [keep.tile([P, T], BF16, name=f"half{j}", tag=f"half{j}") for j in range(2)]
-        nc.vector.tensor_copy(half[0][:], planes[0][:])
+        def vector_gather(i, j):
+            nc.vector.tensor_copy(picked[i][:, :, j], planes[j][:].indirect(offsets(i)))
+
+        def scalar_gather(i, j, window):
+            nc.scalar.activation(picked[i][:, :, j], window[:].indirect(offsets(i)), ACT.Copy)
+
+        half0 = keep.tile([P, T], BF16, name="half0", tag="half0", align_bytes=64)
+        nc.vector.tensor_copy(half0[:], planes[0][:])
+        scalar_gather(0, 0, half0)
+        scalar_gather(1, 0, half0)
+        vector_gather(2, 0)
+        half1 = keep.tile([P, T], BF16, name="half1")
+        nc.vector.tensor_copy(half1[:], planes[1][:])
+        vector_gather(2, 1)
+        w_bf = keep.tile([P, N, PACK], BF16, name="w_bf", tag="half0", align_bytes=64)
+        nc.scalar.activation(w_bf[:], w_raw[:].rearrange("p j n -> p n j"), ACT.Copy)
+        scalar_gather(0, 1, half1)
+        scalar_gather(1, 1, half1)
         for i in range(len(PIECES)):
-            nc.scalar.activation(picked[i][:, :, 0], half[0][:].indirect(offsets(i)), ACT.Copy)
-        w_bf = keep.tile([P, N, PACK], BF16, name="w_bf", align_bytes=64)
-        nc.vector.tensor_copy(w_bf[:], w_raw[:].rearrange("p j n -> p n j"))
+            vector_gather(i, 2)
         w_codes = keep.tile([P, N], U32, name="w_codes", align_bytes=64)
         w_scales = keep.tile([P, N], U8, name="w_scales", align_bytes=64)
         nc.vector.quantize_mx(out=w_codes[:].bitcast(FP8X4), scales=w_scales[:], in_=w_bf[:].rearrange("p n j -> p (n j)"))
-        for i in range(len(PIECES)):
-            nc.vector.tensor_copy(picked[i][:, :, 2], planes[2][:].indirect(offsets(i)))
-        nc.scalar.activation(half[1][:, :CAST_SPLIT], planes[1][:, :CAST_SPLIT], ACT.Copy)
-        nc.vector.tensor_copy(half[1][:, CAST_SPLIT:], planes[1][:, CAST_SPLIT:])
-        for i in range(len(PIECES)):
-            nc.scalar.activation(picked[i][:, :, 1], half[1][:].indirect(offsets(i)), ACT.Copy)
 
         codes = [keep.tile([P, n], U32, name=f"codes{i}", align_bytes=64) for i, (s0, n) in enumerate(PIECES)]
         scales = [keep.tile([P, n], U8, name=f"scales{i}", align_bytes=64) for i, (s0, n) in enumerate(PIECES)]
 
-        def gather_last(i):
-            nc.vector.tensor_copy(picked[i][:, :, 3], planes[3][:].indirect(offsets(i)))
-
         def quantise(i):
             nc.vector.quantize_mx(out=codes[i][:].bitcast(FP8X4), scales=scales[i][:], in_=picked[i][:].rearrange("p n j -> p (n j)"))
 
-        gather_last(0)
-        gather_last(1)
+        vector_gather(0, 3)
+        vector_gather(1, 3)
         quantise(0)
-        gather_last(2)
+        vector_gather(2, 3)
         quantise(1)
         quantise(2)
         attn_all = keep.tile([P, D * V], F32, name="attn_all", tag="picked2", align_bytes=64)
         attn_sb = [attn_all[:, b * 2 * V:(b + 1) * 2 * V] for b in range(2)]
         for b in range(2):
-            nc.vector.tensor_copy(attn_sb[b], attn_banks[b][:])
+            nc.vector.tensor_copy(attn_sb[b].rearrange("p (d n h) -> p d n h", d=2, h=2),
+                                  attn_banks[b][:].rearrange("p (d h n) -> p d n h", d=2, h=2))
 
         y = keep.tile([P, S], F32, name="y")
         for i, (s0, n) in enumerate(PIECES):

@@ -11,7 +11,6 @@ BF16 = mybir.dt.bfloat16
 U32 = mybir.dt.uint32
 U16 = mybir.dt.uint16
 U8 = mybir.dt.uint8
-I32 = mybir.dt.int32
 FP8X4 = mybir.dt.float8_e4m3fn_x4
 ACT = mybir.ActivationFunctionType
 ALU = mybir.AluOpType
@@ -20,8 +19,12 @@ AX = mybir.AxisListType
 P = 128
 PACK = 4
 PER_COL = 16
+PER_PART = V // P
+PER_BANK = 2
 
 PIECES = ((0, 256), (256, 128), (384, 128))
+WIDE, NARROW, OWN = range(len(PIECES))
+SCALAR_CAST = 608
 SCORE_PAD = 8
 
 
@@ -32,20 +35,20 @@ def tile_picked_gatv_none_e_kernel(tc, xT, w1, score, offs, pos1, pos2, pos3, po
         psum = ctx.enter_context(tc.psum_pool(name="psum", bufs=1))
 
         x_rows = xT.rearrange("(p j) t -> p j t", j=PACK)
-        planes = [keep.tile([P, T], F32, name=f"plane{j}") for j in range(PACK)]
+        planes = [keep.tile([P, T], F32, name=f"plane{j}", tag=f"plane{j}", align_bytes=64) for j in range(PACK)]
         offs_sb = keep.tile([P, S // PER_COL], U16, name="offs_sb")
         pos_sb = [keep.tile([P, V // PER_COL], U16, name=f"pos_sb{d}") for d in range(D)]
         w_raw = keep.tile([P, PACK, N], F32, name="w_raw")
         score_sb = keep.tile([P, D, SCORE_PAD], F32, name="score_sb")
         ident = keep.tile([P, P], F32, name="ident")
 
-        nc.scalar.dma_start(score_sb[:, :, 0:2], score[:, 0, :].rearrange("d (p h) -> p d h", h=2))
+        scores = score_sb[:, :, 0:PER_PART]
+        nc.scalar.dma_start(scores, score[:, 0, :].rearrange("d (p h) -> p d h", h=PER_PART))
         nc.sync.dma_start(planes[0][:], x_rows[:, 0, :])
         nc.sync.dma_start(offs_sb[:], offs)
-        for j in (1, 2):
+        for j in (2, 1, 3):
             nc.sync.dma_start(planes[j][:], x_rows[:, j, :])
         nc.sync.dma_start(w_raw[:], w1.rearrange("(p j) n -> p j n", j=PACK))
-        nc.sync.dma_start(planes[3][:], x_rows[:, 3, :])
         for pos_tile, pos in zip(pos_sb, (pos1, pos2, pos3, pos4)):
             nc.sync.dma_start(pos_tile[:], pos)
 
@@ -55,23 +58,27 @@ def tile_picked_gatv_none_e_kernel(tc, xT, w1, score, offs, pos1, pos2, pos3, po
         nc.vector.memset(warm_in[:], 0.0)
         nc.scalar.activation(warm_out[:], warm_in[:], ACT.Exp)
 
-        neg_max = keep.tile([P, 2], F32, name="neg_max")
-        nc.vector.tensor_reduce(neg_max[:], score_sb[:, :, 0:2].rearrange("p d h -> p h d"), AX.X, ALU.max, negate=True)
-        expd = keep.tile([P, 2, D], F32, name="expd")
-        den = keep.tile([P, 2], F32, name="den")
-        for h in range(2):
-            nc.scalar.activation(expd[:, h, :], score_sb[:, :, h], ACT.Exp, bias=neg_max[:, h:h + 1], accum_out=den[:, h:h + 1])
-        inv_den = keep.tile([P, 2], F32, name="inv_den")
+        neg_max = keep.tile([P, PER_PART], F32, name="neg_max")
+        nc.vector.tensor_reduce(neg_max[:], scores.rearrange("p d h -> p h d"), AX.X, ALU.max, negate=True)
+        expd = keep.tile([P, PER_PART, D], F32, name="expd")
+        den = keep.tile([P, PER_PART], F32, name="den")
+        for h in range(PER_PART):
+            nc.scalar.activation(expd[:, h, :], score_sb[:, :, h], ACT.Exp,
+                                 bias=neg_max[:, h:h + 1], accum_out=den[:, h:h + 1])
+        inv_den = keep.tile([P, PER_PART], F32, name="inv_den")
         nc.vector.reciprocal(inv_den[:], den[:])
-        attn = keep.tile([P, 2, D], F32, name="attn")
-        nc.vector.tensor_tensor(attn[:], expd[:], inv_den[:].unsqueeze(2).to_broadcast([P, 2, D]), ALU.mult)
-        attn_banks = [psum.tile([P, 2 * V], F32, name=f"attn_bank{b}") for b in range(2)]
-        for d in range(D):
-            for h in range(2):
-                c0 = (d % 2) * V + h * P
-                nc.tensor.transpose(attn_banks[d // 2][:, c0:c0 + P], attn[:, h, d:d + 1].to_broadcast([P, P]), ident[:])
+        attn = keep.tile([P, PER_PART, D], F32, name="attn")
+        nc.vector.tensor_tensor(attn[:], expd[:], inv_den[:].unsqueeze(2).to_broadcast([P, PER_PART, D]), ALU.mult)
 
-        picked = [keep.tile([P, n, PACK], BF16, name=f"picked{i}", tag=f"picked{i}", align_bytes=64) for i, (s0, n) in enumerate(PIECES)]
+        attn_banks = [psum.tile([P, PER_BANK * V], F32, name=f"attn_bank{b}") for b in range(D // PER_BANK)]
+        for d in range(D):
+            for h in range(PER_PART):
+                c0 = (d % PER_BANK) * V + h * P
+                nc.tensor.transpose(attn_banks[d // PER_BANK][:, c0:c0 + P],
+                                    attn[:, h, d:d + 1].to_broadcast([P, P]), ident[:])
+
+        picked = [keep.tile([P, n, PACK], BF16, name=f"picked{i}", tag=f"picked{i}", align_bytes=64)
+                  for i, (s0, n) in enumerate(PIECES)]
 
         def offsets(i):
             s0, n = PIECES[i]
@@ -81,69 +88,75 @@ def tile_picked_gatv_none_e_kernel(tc, xT, w1, score, offs, pos1, pos2, pos3, po
             nc.vector.tensor_copy(picked[i][:, :, j], planes[j][:].indirect(offsets(i)))
 
         def scalar_gather(i, j, window):
-            nc.scalar.activation(picked[i][:, :, j], window[:].indirect(offsets(i)), ACT.Copy)
+            nc.scalar.activation(picked[i][:, :, j], window.indirect(offsets(i)), ACT.Copy)
 
-        half0 = keep.tile([P, T], BF16, name="half0", tag="half0", align_bytes=64)
-        nc.vector.tensor_copy(half0[:], planes[0][:])
-        scalar_gather(0, 0, half0)
-        scalar_gather(1, 0, half0)
-        vector_gather(2, 0)
-        half1 = keep.tile([P, T], BF16, name="half1")
-        nc.vector.tensor_copy(half1[:], planes[1][:])
-        vector_gather(2, 1)
-        w_bf = keep.tile([P, N, PACK], BF16, name="w_bf", tag="half0", align_bytes=64)
-        nc.scalar.activation(w_bf[:], w_raw[:].rearrange("p j n -> p n j"), ACT.Copy)
-        scalar_gather(0, 1, half1)
-        scalar_gather(1, 1, half1)
+        rounded = keep.tile([P, 2 * T - SCALAR_CAST], BF16, name="rounded", tag="rounded")
+        rounded0 = rounded[:, :T]
+        rounded1 = rounded[:, T - SCALAR_CAST:]
+        nc.vector.tensor_copy(rounded0, planes[0][:])
+        scalar_gather(WIDE, 0, rounded0)
+        scalar_gather(NARROW, 0, rounded0)
+        vector_gather(OWN, 0)
         for i in range(len(PIECES)):
             vector_gather(i, 2)
-        w_codes = keep.tile([P, N], U32, name="w_codes", align_bytes=64)
-        w_scales = keep.tile([P, N], U8, name="w_scales", align_bytes=64)
-        nc.vector.quantize_mx(out=w_codes[:].bitcast(FP8X4), scales=w_scales[:], in_=w_bf[:].rearrange("p n j -> p (n j)"))
+        nc.scalar.activation(rounded1[:, :SCALAR_CAST], planes[1][:, :SCALAR_CAST], ACT.Copy)
+        nc.vector.tensor_copy(rounded1[:, SCALAR_CAST:], planes[1][:, SCALAR_CAST:])
+        vector_gather(OWN, 1)
+        scalar_gather(WIDE, 1, rounded1)
+        w_bf = keep.tile([P, N, PACK], BF16, name="w_bf", tag="plane1", align_bytes=64)
+        nc.scalar.activation(w_bf[:], w_raw[:].rearrange("p j n -> p n j"), ACT.Copy)
+        scalar_gather(NARROW, 1, rounded1)
+        for i in (OWN, WIDE, NARROW):
+            vector_gather(i, 3)
 
         codes = [keep.tile([P, n], U32, name=f"codes{i}", align_bytes=64) for i, (s0, n) in enumerate(PIECES)]
         scales = [keep.tile([P, n], U8, name=f"scales{i}", align_bytes=64) for i, (s0, n) in enumerate(PIECES)]
+        w_codes = keep.tile([P, N], U32, name="w_codes", align_bytes=64)
+        w_scales = keep.tile([P, N], U8, name="w_scales", align_bytes=64)
 
-        def quantise(i):
-            nc.vector.quantize_mx(out=codes[i][:].bitcast(FP8X4), scales=scales[i][:], in_=picked[i][:].rearrange("p n j -> p (n j)"))
+        def quantise(code_tile, scale_tile, src):
+            nc.vector.quantize_mx(out=code_tile[:].bitcast(FP8X4), scales=scale_tile[:],
+                                  in_=src[:].rearrange("p n j -> p (n j)"))
 
-        vector_gather(0, 3)
-        vector_gather(1, 3)
-        quantise(0)
-        vector_gather(2, 3)
-        quantise(1)
-        quantise(2)
-        attn_all = keep.tile([P, D * V], F32, name="attn_all", tag="picked2", align_bytes=64)
-        attn_sb = [attn_all[:, b * 2 * V:(b + 1) * 2 * V] for b in range(2)]
-        for b in range(2):
-            nc.vector.tensor_copy(attn_sb[b].rearrange("p (d n h) -> p d n h", d=2, h=2),
-                                  attn_banks[b][:].rearrange("p (d h n) -> p d n h", d=2, h=2))
+        quantise(codes[OWN], scales[OWN], picked[OWN])
+        quantise(codes[WIDE], scales[WIDE], picked[WIDE])
+        quantise(w_codes, w_scales, w_bf)
+        quantise(codes[NARROW], scales[NARROW], picked[NARROW])
+
+        attn_sb = [keep.tile([P, PER_BANK * V], F32, name="attn_sb0", tag="rounded"),
+                   keep.tile([P, PER_BANK * V], F32, name="attn_sb1", tag=f"picked{NARROW}", align_bytes=64)]
+        for b, copy in enumerate((nc.scalar.copy, nc.vector.tensor_copy)):
+            copy(attn_sb[b][:].rearrange("m (d p h) -> m d p h", d=PER_BANK, h=PER_PART),
+                 attn_banks[b][:].rearrange("m (d h p) -> m d p h", d=PER_BANK, h=PER_PART))
 
         y = keep.tile([P, S], F32, name="y")
-        for i, (s0, n) in enumerate(PIECES):
+        for i in (WIDE, OWN, NARROW):
+            s0, n = PIECES[i]
             acc = psum.tile([P, n], F32, name=f"acc{i}")
             nc.tensor.matmul_mx(out=acc[:], lhsT=w_codes[:].bitcast(FP8X4), lhsT_scale=w_scales[:],
                                 rhs=codes[i][:].bitcast(FP8X4), rhs_scale=scales[i][:], start=True, stop=True)
-            nc.scalar.copy(y[:, s0:s0 + n], acc[:])
+            copy = nc.vector.tensor_copy if i == NARROW else nc.scalar.copy
+            copy(y[:, s0:s0 + n], acc[:])
 
         terms = [keep.tile([P, V], F32, name=f"term{d}") for d in range(D)]
 
         def weighted(d, c0, n):
-            a0 = (d % 2) * V + c0
-            nc.vector.tensor_tensor(terms[d][:, c0:c0 + n], y[:].indirect(pos_sb[d][:, c0 // PER_COL:(c0 + n) // PER_COL]),
-                                    attn_sb[d // 2][:, a0:a0 + n], ALU.mult)
+            a0 = (d % PER_BANK) * V + c0
+            neighbours = y[:].indirect(pos_sb[d][:, c0 // PER_COL:(c0 + n) // PER_COL])
+            nc.vector.tensor_tensor(terms[d][:, c0:c0 + n], neighbours, attn_sb[d // PER_BANK][:, a0:a0 + n], ALU.mult)
 
+        half_v = V // 2
         sum01 = keep.tile([P, V], F32, name="sum01")
         sum012 = keep.tile([P, V], F32, name="sum012")
-        res = [keep.tile([P, P], F32, name=f"res{h}") for h in range(2)]
+        res = [keep.tile([P, half_v], F32, name=f"res{u}") for u in range(2)]
         weighted(0, 0, V)
         weighted(1, 0, V)
         weighted(2, 0, V)
         nc.vector.tensor_tensor(sum01[:], terms[0][:], terms[1][:], ALU.add)
-        weighted(3, 0, P)
+        weighted(3, 0, half_v)
         nc.vector.tensor_tensor(sum012[:], sum01[:], terms[2][:], ALU.add)
-        weighted(3, P, P)
-        for h in range(2):
-            cols = slice(h * P, (h + 1) * P)
-            nc.vector.tensor_tensor(res[h][:], sum012[:, cols], terms[3][:, cols], ALU.add)
-            (nc.scalar if h == 0 else nc.sync).dma_start(out[:, cols], res[h][:])
+        weighted(3, half_v, half_v)
+        for u, queue in enumerate((nc.scalar, nc.sync)):
+            cols = slice(u * half_v, (u + 1) * half_v)
+            nc.vector.tensor_tensor(res[u][:], sum012[:, cols], terms[3][:, cols], ALU.add)
+            queue.dma_start(out[:, cols], res[u][:])

from contextlib import ExitStack

import concourse.mybir as mybir
from concourse.masks import make_identity

K, T, S, D, V, N = 512, 1024, 512, 4, 256, 128
FLOPS = 2 * K * S * N

F32 = mybir.dt.float32
BF16 = mybir.dt.bfloat16
U32 = mybir.dt.uint32
U16 = mybir.dt.uint16
U8 = mybir.dt.uint8
FP8X4 = mybir.dt.float8_e4m3fn_x4
ACT = mybir.ActivationFunctionType
ALU = mybir.AluOpType
AX = mybir.AxisListType

P = 128
PACK = 4
PER_COL = 16
PER_PART = V // P
PER_BANK = 2

PIECES = ((0, 256), (256, 128), (384, 128))
WIDE, NARROW, OWN = range(len(PIECES))
SCALAR_CAST = 608
SCORE_PAD = 8


def tile_picked_gatv_none_e_kernel(tc, xT, w1, score, offs, pos1, pos2, pos3, pos4, out):
    nc = tc.nc
    with ExitStack() as ctx:
        keep = ctx.enter_context(tc.tile_pool(name="keep", bufs=1))
        psum = ctx.enter_context(tc.psum_pool(name="psum", bufs=1))

        x_rows = xT.rearrange("(p j) t -> p j t", j=PACK)
        planes = [keep.tile([P, T], F32, name=f"plane{j}", tag=f"plane{j}", align_bytes=64) for j in range(PACK)]
        offs_sb = keep.tile([P, S // PER_COL], U16, name="offs_sb")
        pos_sb = [keep.tile([P, V // PER_COL], U16, name=f"pos_sb{d}") for d in range(D)]
        w_raw = keep.tile([P, PACK, N], F32, name="w_raw")
        score_sb = keep.tile([P, D, SCORE_PAD], F32, name="score_sb")
        ident = keep.tile([P, P], F32, name="ident")

        scores = score_sb[:, :, 0:PER_PART]
        nc.scalar.dma_start(scores, score[:, 0, :].rearrange("d (p h) -> p d h", h=PER_PART))
        nc.sync.dma_start(planes[0][:], x_rows[:, 0, :])
        nc.sync.dma_start(offs_sb[:], offs)
        for j in (2, 1, 3):
            nc.sync.dma_start(planes[j][:], x_rows[:, j, :])
        nc.sync.dma_start(w_raw[:], w1.rearrange("(p j) n -> p j n", j=PACK))
        for pos_tile, pos in zip(pos_sb, (pos1, pos2, pos3, pos4)):
            nc.sync.dma_start(pos_tile[:], pos)

        make_identity(nc, ident[:])
        warm_in = keep.tile([P, 1], F32, name="warm_in")
        warm_out = keep.tile([P, 1], F32, name="warm_out")
        nc.vector.memset(warm_in[:], 0.0)
        nc.scalar.activation(warm_out[:], warm_in[:], ACT.Exp)

        neg_max = keep.tile([P, PER_PART], F32, name="neg_max")
        nc.vector.tensor_reduce(neg_max[:], scores.rearrange("p d h -> p h d"), AX.X, ALU.max, negate=True)
        expd = keep.tile([P, PER_PART, D], F32, name="expd")
        den = keep.tile([P, PER_PART], F32, name="den")
        for h in range(PER_PART):
            nc.scalar.activation(expd[:, h, :], score_sb[:, :, h], ACT.Exp,
                                 bias=neg_max[:, h:h + 1], accum_out=den[:, h:h + 1])
        inv_den = keep.tile([P, PER_PART], F32, name="inv_den")
        nc.vector.reciprocal(inv_den[:], den[:])
        attn = keep.tile([P, PER_PART, D], F32, name="attn")
        nc.vector.tensor_tensor(attn[:], expd[:], inv_den[:].unsqueeze(2).to_broadcast([P, PER_PART, D]), ALU.mult)

        attn_banks = [psum.tile([P, PER_BANK * V], F32, name=f"attn_bank{b}") for b in range(D // PER_BANK)]
        for d in range(D):
            for h in range(PER_PART):
                c0 = (d % PER_BANK) * V + h * P
                nc.tensor.transpose(attn_banks[d // PER_BANK][:, c0:c0 + P],
                                    attn[:, h, d:d + 1].to_broadcast([P, P]), ident[:])

        picked = [keep.tile([P, n, PACK], BF16, name=f"picked{i}", tag=f"picked{i}", align_bytes=64)
                  for i, (s0, n) in enumerate(PIECES)]

        def offsets(i):
            s0, n = PIECES[i]
            return offs_sb[:, s0 // PER_COL:(s0 + n) // PER_COL]

        def vector_gather(i, j):
            nc.vector.tensor_copy(picked[i][:, :, j], planes[j][:].indirect(offsets(i)))

        def scalar_gather(i, j, window):
            nc.scalar.activation(picked[i][:, :, j], window.indirect(offsets(i)), ACT.Copy)

        rounded = keep.tile([P, 2 * T - SCALAR_CAST], BF16, name="rounded", tag="rounded")
        rounded0 = rounded[:, :T]
        rounded1 = rounded[:, T - SCALAR_CAST:]
        nc.vector.tensor_copy(rounded0, planes[0][:])
        scalar_gather(WIDE, 0, rounded0)
        scalar_gather(NARROW, 0, rounded0)
        vector_gather(OWN, 0)
        for i in range(len(PIECES)):
            vector_gather(i, 2)
        nc.scalar.activation(rounded1[:, :SCALAR_CAST], planes[1][:, :SCALAR_CAST], ACT.Copy)
        nc.vector.tensor_copy(rounded1[:, SCALAR_CAST:], planes[1][:, SCALAR_CAST:])
        vector_gather(OWN, 1)
        scalar_gather(WIDE, 1, rounded1)
        w_bf = keep.tile([P, N, PACK], BF16, name="w_bf", tag="plane1", align_bytes=64)
        nc.scalar.activation(w_bf[:], w_raw[:].rearrange("p j n -> p n j"), ACT.Copy)
        scalar_gather(NARROW, 1, rounded1)
        for i in (OWN, WIDE, NARROW):
            vector_gather(i, 3)

        codes = [keep.tile([P, n], U32, name=f"codes{i}", align_bytes=64) for i, (s0, n) in enumerate(PIECES)]
        scales = [keep.tile([P, n], U8, name=f"scales{i}", align_bytes=64) for i, (s0, n) in enumerate(PIECES)]
        w_codes = keep.tile([P, N], U32, name="w_codes", align_bytes=64)
        w_scales = keep.tile([P, N], U8, name="w_scales", align_bytes=64)

        def quantise(code_tile, scale_tile, src):
            nc.vector.quantize_mx(out=code_tile[:].bitcast(FP8X4), scales=scale_tile[:],
                                  in_=src[:].rearrange("p n j -> p (n j)"))

        quantise(codes[OWN], scales[OWN], picked[OWN])
        quantise(codes[WIDE], scales[WIDE], picked[WIDE])
        quantise(w_codes, w_scales, w_bf)
        quantise(codes[NARROW], scales[NARROW], picked[NARROW])

        attn_sb = [keep.tile([P, PER_BANK * V], F32, name="attn_sb0", tag="rounded"),
                   keep.tile([P, PER_BANK * V], F32, name="attn_sb1", tag=f"picked{NARROW}", align_bytes=64)]
        for b, copy in enumerate((nc.scalar.copy, nc.vector.tensor_copy)):
            copy(attn_sb[b][:].rearrange("m (d p h) -> m d p h", d=PER_BANK, h=PER_PART),
                 attn_banks[b][:].rearrange("m (d h p) -> m d p h", d=PER_BANK, h=PER_PART))

        y = keep.tile([P, S], F32, name="y")
        for i in (WIDE, OWN, NARROW):
            s0, n = PIECES[i]
            acc = psum.tile([P, n], F32, name=f"acc{i}")
            nc.tensor.matmul_mx(out=acc[:], lhsT=w_codes[:].bitcast(FP8X4), lhsT_scale=w_scales[:],
                                rhs=codes[i][:].bitcast(FP8X4), rhs_scale=scales[i][:], start=True, stop=True)
            copy = nc.vector.tensor_copy if i == NARROW else nc.scalar.copy
            copy(y[:, s0:s0 + n], acc[:])

        terms = [keep.tile([P, V], F32, name=f"term{d}") for d in range(D)]

        def weighted(d, c0, n):
            a0 = (d % PER_BANK) * V + c0
            neighbours = y[:].indirect(pos_sb[d][:, c0 // PER_COL:(c0 + n) // PER_COL])
            nc.vector.tensor_tensor(terms[d][:, c0:c0 + n], neighbours, attn_sb[d // PER_BANK][:, a0:a0 + n], ALU.mult)

        half_v = V // 2
        sum01 = keep.tile([P, V], F32, name="sum01")
        sum012 = keep.tile([P, V], F32, name="sum012")
        res = [keep.tile([P, half_v], F32, name=f"res{u}") for u in range(2)]
        weighted(0, 0, V)
        weighted(1, 0, V)
        weighted(2, 0, V)
        nc.vector.tensor_tensor(sum01[:], terms[0][:], terms[1][:], ALU.add)
        weighted(3, 0, half_v)
        nc.vector.tensor_tensor(sum012[:], sum01[:], terms[2][:], ALU.add)
        weighted(3, half_v, half_v)
        for u, queue in enumerate((nc.scalar, nc.sync)):
            cols = slice(u * half_v, (u + 1) * half_v)
            nc.vector.tensor_tensor(res[u][:], sum012[:, cols], terms[3][:, cols], ALU.add)
            queue.dma_start(out[:, cols], res[u][:])
